import numpy as np
import ml_dtypes


def mxq(x, axis, fmt="e4m3"):
    dtype, down = {"e4m3": (ml_dtypes.float8_e4m3fn, 7), "e5m2": (ml_dtypes.float8_e5m2, 14)}[fmt]
    v = np.moveaxis(np.asarray(x, np.float32).astype(ml_dtypes.bfloat16).astype(np.float64), axis, -1)
    blocks = v.reshape(v.shape[:-1] + (-1, 32))
    amax = np.abs(blocks).max(-1, keepdims=True)
    byte = np.maximum(np.where(amax > 0, np.frexp(amax)[1] - 1 + 127, 0) - down, 1)
    scale = np.exp2(byte - 127.0)
    codes = (blocks / scale).astype(np.float32).astype(dtype).astype(np.float64)
    return np.moveaxis((codes * scale).reshape(v.shape), -1, axis)


WIDE = False


def mx_kscale(k):
    if not WIDE:
        return np.ones(k)
    levels = np.array([30, -30])
    if k % 512:
        return np.exp2(np.random.permutation(np.resize(levels, k // 32))).repeat(32)
    a = np.empty((k // 512, 16))
    for p in range(k // 512):
        a[p, :8] = np.random.permutation(np.resize(levels, 8))
        for g in range(8):
            far = levels[np.abs(levels - a[p, g]) >= 10]
            a[p, g + 8] = far[np.random.randint(len(far))]
    return np.exp2(a.ravel()).repeat(32)


def f64(x):
    return np.asarray(x).astype(np.float64)


def striped(idx):
    return np.tile(np.asarray(idx).reshape(-1, 16).T, (8, 1)).astype(np.uint16)


def unstriped(offs):
    return offs[:16].T.reshape(-1).astype(np.int64)


def striped8(idx):
    return np.asarray(idx).reshape(8, -1, 16).transpose(0, 2, 1).reshape(128, -1).astype(np.uint16)


def unstriped8(offs):
    return offs.reshape(8, 16, -1).transpose(0, 2, 1).reshape(8, -1).astype(np.int64)


def pick8(x, idx, run):
    r = np.arange(len(x))
    return x[r[:, None], idx[r % (8 * run) // run]]


E2M1 = np.array([0.0, 0.5, 1.0, 1.5, 2.0, 3.0, 4.0, 6.0, -0.0, -0.5, -1.0, -1.5, -2.0, -3.0, -4.0, -6.0])


def pack_weight(w, fmt):
    k, n = w.shape
    w = f64(np.asarray(w, np.float32).astype(ml_dtypes.bfloat16)).reshape(k // 32, 32, n)
    amax = np.abs(w).max(1)
    if fmt in ("e4m3", "e5m2"):
        byte = np.frexp(amax)[1] - 1 + 127 - (7 if fmt == "e4m3" else 14)
    else:
        mant, ex = np.frexp(amax / 6.0)
        byte = np.where(mant > 0.5, ex, ex - 1) + 127
    byte = np.clip(np.where(amax > 0, byte, 1), 1, 254)
    scaled = (w * np.exp2(127.0 - byte)[:, None, :]).reshape(k, n).astype(np.float32)
    by_word = np.ascontiguousarray(scaled.reshape(k // 512, 128, 4, n).transpose(0, 1, 3, 2))
    if fmt in ("e4m3", "e5m2"):
        words = by_word.astype(ml_dtypes.float8_e4m3fn if fmt == "e4m3" else ml_dtypes.float8_e5m2).view(np.uint8)
    else:
        c = by_word.astype(ml_dtypes.float4_e2m1fn).view(np.uint8) & 0xF
        words = (c[..., 0::2] | (c[..., 1::2] << 4)).reshape(k // 512, 128, 2 * n)
    return np.ascontiguousarray(words), np.ascontiguousarray(byte.astype(np.uint8).reshape(k // 512, 16, n))


def unpack_weight(words, scales, fmt):
    g, _, n = scales.shape
    words = np.ascontiguousarray(words).reshape(g, 128, n, -1)
    if fmt in ("e4m3", "e5m2"):
        vals = words.view(ml_dtypes.float8_e4m3fn if fmt == "e4m3" else ml_dtypes.float8_e5m2).astype(np.float64)
    else:
        nib = np.empty((g, 128, n, 4), np.uint8)
        nib[..., 0::2] = words & 0xF
        nib[..., 1::2] = words >> 4
        vals = E2M1[nib]
    vals = vals * np.repeat(np.exp2(scales.astype(np.float64) - 127.0), 8, axis=1)[..., None]
    return vals.transpose(0, 1, 3, 2).reshape(g * 512, n)


K, T, J, R, C, O, N, S, E = 512, 1024, 256, 512, 512, 128, 256, 1024, 1024


def setup_inputs():
    n = np.random.standard_normal
    idx = np.random.permutation(T)[:J]
    idx2 = np.stack([np.random.permutation(C)[:J] for _ in range(8)])
    idx3 = np.random.permutation(C)[:J]
    idx4 = np.random.permutation(J)[:O]
    idx5 = np.random.permutation(J)[:O]
    idx6 = np.random.permutation(S)[:N]
    idx7 = np.random.permutation(E)[:O]
    fk = mx_kscale(K)
    fr = mx_kscale(R)
    xtp = pack_weight(n((K, T)) / fk[:, None], "e4m3")
    wp = pack_weight(n((K, R)) * 1 / np.sqrt(K) * fk[:, None] * fr, "e2m1")
    w2p = pack_weight(n((K, R)) * 1 / np.sqrt(K) * fk[:, None] * fr, "e5m2")
    vsp = pack_weight(n((R, S)) * 1 / np.sqrt(R) / fr[:, None], "e5m2")
    return {
        "xt_words": xtp[0],
        "xt_scales": xtp[1],
        "w_words": wp[0],
        "w_scales": wp[1],
        "w2_words": w2p[0],
        "w2_scales": w2p[1],
        "sa": (np.random.uniform(0.5, 1.6, (R, 1))).astype(np.float32),
        "sb": (np.random.uniform(0.5, 1.6, (R, 1))).astype(np.float32),
        "vs_words": vsp[0],
        "vs_scales": vsp[1],
        "offs": striped(idx),
        "offs2": striped8(idx2),
        "offs3": striped(idx3),
        "offs4": striped(idx4),
        "offs5": striped(idx5),
        "offs6": striped(idx6),
        "offs7": striped(idx7),
    }


def reference(xt_words, xt_scales, w_words, w_scales, w2_words, w2_scales, sa, sb, vs_words, vs_scales, offs, offs2, offs3, offs4, offs5, offs6, offs7):
    idx = unstriped(offs)
    idx2 = unstriped8(offs2)
    idx3 = unstriped(offs3)
    idx4 = unstriped(offs4)
    idx5 = unstriped(offs5)
    idx6 = unstriped(offs6)
    idx7 = unstriped(offs7)
    xtu = unpack_weight(xt_words, xt_scales, "e4m3")
    wu = unpack_weight(w_words, w_scales, "e2m1")
    w2u = unpack_weight(w2_words, w2_scales, "e5m2")
    vsu = unpack_weight(vs_words, vs_scales, "e5m2")
    xtidxg = xtu[:, idx]
    a = wu.T @ xtidxg
    b = w2u.T @ xtidxg
    pw = np.zeros((R, C))
    pw[np.arange(R)[:, None], idx2[np.arange(R) % 512 // 64]] = a
    rb = np.maximum(pw[:, idx3] * f64(sa), b)
    hid = np.abs(rb[:, idx4] - rb[:, idx5] * f64(sb))
    vsidx6g = vsu[:, idx6]
    hidq = mxq(hid, 0, "e4m3")
    p = vsidx6g.T @ hidq
    y = np.zeros((N, E))
    y[:, idx7] = p
    return y

@@ -1,0 +1,211 @@
+from contextlib import ExitStack
+
+import concourse.mybir as mybir
+
+K, T, J, R, C, O, N, S, E = 512, 1024, 256, 512, 512, 128, 256, 1024, 1024
+FLOPS = 2 * (2 * K * R * J + R * N * O)
+
+F32 = mybir.dt.float32
+BF16 = mybir.dt.bfloat16
+I32 = mybir.dt.int32
+U32 = mybir.dt.uint32
+U16 = mybir.dt.uint16
+U8 = mybir.dt.uint8
+E4M3 = mybir.dt.float8_e4m3fn_x4
+E5M2 = mybir.dt.float8_e5m2_x4
+E2M1 = mybir.dt.float4_e2m1fn_x4
+COPY = mybir.ActivationFunctionType.Copy
+ALU = mybir.AluOpType
+
+P = 128
+PACK = 4
+QUADS = 4
+QUAD = 32
+
+
+def load_list(nc, pool, src, name):
+    t = pool.tile(list(src.shape), U16, name=name)
+    nc.sync.dma_start(t[:], src)
+    return t
+
+
+def load_scale_rows(nc, pool, scales, name):
+    rows = pool.tile([PACK, QUADS, scales.shape[2] // 4], I32, name=name)
+    nc.sync.dma_start(rows[:], scales[0].bitcast(I32).rearrange("(q r) n -> r q n", r=PACK))
+    return rows
+
+
+def spread_scale_rows(nc, plane, rows):
+    for q in range(QUADS):
+        nc.vector.tensor_copy(plane[QUAD * q : QUAD * q + PACK, :].bitcast(I32), rows[:, q, :])
+
+
+def tile_list_ownanswer_twow_store_scattered_kernel(
+    tc, xt_words, xt_scales, w_words, w_scales, w2_words, w2_scales, sa, sb, vs_words, vs_scales,
+    offs, offs2, offs3, offs4, offs5, offs6, offs7, out,
+):
+    nc = tc.nc
+    with ExitStack() as ctx:
+        keep = ctx.enter_context(tc.tile_pool(name="keep", bufs=1))
+        psum = ctx.enter_context(tc.psum_pool(name="psum", bufs=1))
+
+        xs = keep.tile([P, T], U8, name="xs", align_bytes=64)
+        ws = keep.tile([P, R], U8, name="ws", align_bytes=64)
+        boards = [keep.tile([P, C], F32, name="board%d" % t) for t in range(PACK)]
+        nc.vector.memset(xs[:].bitcast(I32), 0)
+        nc.vector.memset(ws[:].bitcast(I32), 0)
+        nc.vector.memset(boards[0][:], 0.0)
+        for t in range(1, PACK):
+            nc.vector.memset(boards[t][:], 0.0)
+
+        xw = keep.tile([P, T], U32, name="xw", align_bytes=64)
+        nc.scalar.dma_start(xw[:].bitcast(I32), xt_words[0].rearrange("p n t -> p (n t)").bitcast(I32))
+        xs_rows = load_scale_rows(nc, keep, xt_scales, "xs_rows")
+        ws_rows = load_scale_rows(nc, keep, w_scales, "ws_rows")
+        l1 = load_list(nc, keep, offs, "l1")
+        ww = keep.tile([P, R], U16, name="ww", align_bytes=64)
+        nc.sync.dma_start(ww[:].bitcast(I32), w_words[0].bitcast(I32))
+        l2 = load_list(nc, keep, offs2, "l2")
+        l3 = load_list(nc, keep, offs3, "l3")
+        sa_t = keep.tile([P, PACK], F32, name="sa_t")
+        nc.sync.dma_start(sa_t[:], sa.rearrange("(p t) o -> p (t o)", t=PACK))
+        w2s_rows = load_scale_rows(nc, keep, w2_scales, "w2s_rows")
+        w2w = keep.tile([P, R], U32, name="w2w", tag="wide1", align_bytes=64)
+        nc.sync.dma_start(w2w[:].bitcast(I32), w2_words[0].rearrange("p n t -> p (n t)").bitcast(I32))
+        vss_rows = load_scale_rows(nc, keep, vs_scales, "vss_rows")
+        l6 = load_list(nc, keep, offs6, "l6")
+        vw = keep.tile([P, S], U32, name="vw", tag="wide2", align_bytes=64)
+        nc.sync.dma_start(vw[:].bitcast(I32), vs_words[0].rearrange("p n t -> p (n t)").bitcast(I32))
+        l4 = load_list(nc, keep, offs4, "l4")
+        l5 = load_list(nc, keep, offs5, "l5")
+        sb_t = keep.tile([P, PACK], F32, name="sb_t")
+        nc.sync.dma_start(sb_t[:], sb.rearrange("(p t) o -> p (t o)", t=PACK))
+        l7 = load_list(nc, keep, offs7, "l7")
+
+        spread_scale_rows(nc, xs, xs_rows)
+        spread_scale_rows(nc, ws, ws_rows)
+        wsd = keep.tile([P, PACK, P], U8, name="wsd", tag="chain_s", align_bytes=64)
+        nc.vector.tensor_copy(wsd[:], ws[:].rearrange("p (m t) -> p t m", t=PACK))
+        wwd = keep.tile([P, PACK, P], U16, name="wwd", tag="chain_w", align_bytes=64)
+        nc.scalar.copy(wwd[:], ww[:].rearrange("p (m t) -> p t m", t=PACK))
+
+        xgs = keep.tile([P, J], U8, name="xgs", align_bytes=64)
+        xgw = keep.tile([P, J], U32, name="xgw", align_bytes=64)
+        half = J // 2
+        halves = [(slice(0, half), slice(0, half // 16)), (slice(half, J), slice(half // 16, J // 16))]
+        for cols, entries in halves:
+            nc.vector.tensor_copy(xgs[:, cols], xs[:].indirect(l1[:, entries]))
+            nc.vector.tensor_copy(xgw[:, cols], xw[:].indirect(l1[:, entries]))
+
+        a_sb = keep.tile([P, PACK, J], F32, name="a_sb")
+
+        def first_product(bank, t, cols):
+            nc.tensor.matmul_mx(
+                bank, lhsT=wwd[:, t, :].bitcast(E2M1), lhsT_scale=wsd[:, t, :],
+                rhs=xgw[:, cols].bitcast(E4M3), rhs_scale=xgs[:, cols], start=True, stop=True,
+            )
+
+        for u, (cols, entries) in enumerate(halves):
+            bank = psum.tile([P, half], F32, name="a_ps0%d" % u)
+            first_product(bank[:], 0, cols)
+            nc.vector.tensor_copy(a_sb[:, 0, cols], bank[:])
+        bank = psum.tile([P, J], F32, name="a_ps1")
+        first_product(bank[:], 1, slice(0, J))
+        nc.vector.tensor_copy(a_sb[:, 1, :], bank[:])
+        bank = psum.tile([P, 2, J], F32, name="a_ps23")
+        for t in (2, 3):
+            first_product(bank[:, t - 2, :], t, slice(0, J))
+        nc.vector.tensor_copy(a_sb[:, 2:4, :], bank[:])
+
+        w2s = keep.tile([P, R], U8, name="w2s", tag="chain_s", align_bytes=64)
+        nc.vector.memset(w2s[:].bitcast(I32), 0)
+        spread_scale_rows(nc, w2s, w2s_rows)
+        w2sd = keep.tile([P, PACK, P], U8, name="w2sd", align_bytes=64)
+        nc.vector.tensor_copy(w2sd[:], w2s[:].rearrange("p (m t) -> p t m", t=PACK))
+        w2wd = keep.tile([P, PACK, P], U32, name="w2wd", tag="chain_w", align_bytes=64)
+        nc.vector.tensor_copy(w2wd[:], w2w[:].rearrange("p (m t) -> p t m", t=PACK))
+        b_ps = []
+        b_banks = [psum.tile([P, 2, J], F32, name="b_ps%d" % u) for u in range(2)]
+        for t in range(PACK):
+            bank = b_banks[t // 2][:, t % 2, :]
+            nc.tensor.matmul_mx(
+                bank, lhsT=w2wd[:, t, :].bitcast(E5M2), lhsT_scale=w2sd[:, t, :],
+                rhs=xgw[:].bitcast(E4M3), rhs_scale=xgs[:], start=True, stop=True,
+            )
+            b_ps.append(bank)
+
+        pages = []
+        page0 = keep.tile([P, E], F32, name="page0", tag="chain_w", align_bytes=64)
+        nc.vector.memset(page0[:], 0.0)
+        pages.append(page0)
+        vgs = keep.tile([P, N], U8, name="vgs", align_bytes=64)
+        vgw = keep.tile([P, N], U32, name="vgw", tag="chain_s", align_bytes=64)
+
+        vss = keep.tile([P, S], U8, name="vss", tag="wide1", align_bytes=64)
+        nc.vector.memset(vss[:].bitcast(I32), 0)
+        spread_scale_rows(nc, vss, vss_rows)
+        nc.vector.tensor_copy(vgs[:], vss[:].indirect(l6[:]))
+        nc.vector.tensor_copy(vgw[:], vw[:].indirect(l6[:]))
+
+        page1 = keep.tile([P, E], F32, name="page1", tag="wide1", align_bytes=64)
+        nc.vector.memset(page1[:], 0.0)
+        pages.append(page1)
+        first = keep.tile([P, PACK, O], F32, name="first")
+        second = keep.tile([P, PACK, O], F32, name="second")
+        diff = keep.tile([P, PACK, O], F32, name="diff")
+        rb = [keep.tile([P, J], F32, name="rb0", tag="wide2", align_bytes=64)]
+        rb.extend(keep.tile([P, J], F32, name="rb%d" % t) for t in range(1, PACK))
+
+        def put(t):
+            if t == 0:
+                for cols, entries in halves:
+                    nc.scalar.activation(boards[t][:].indirect(l2[:, entries]), a_sb[:, t, cols], COPY)
+            else:
+                nc.scalar.activation(boards[t][:].indirect(l2[:]), a_sb[:, t, :], COPY)
+
+        def answer(t):
+            looked = keep.tile([P, J], F32, name="looked%d" % t)
+            nc.scalar.activation(looked[:], boards[t][:].indirect(l3[:]), COPY, scale=sa_t[:, t : t + 1])
+            nc.vector.tensor_tensor(rb[t][:], b_ps[t], looked[:], ALU.max)
+            nc.vector.tensor_copy(first[:, t, :], rb[t][:].indirect(l4[:]))
+
+        def differ(t):
+            nc.scalar.activation(second[:, t, :], rb[t][:].indirect(l5[:]), COPY, scale=sb_t[:, t : t + 1])
+            nc.vector.tensor_tensor(diff[:, t, :], first[:, t, :], second[:, t, :], ALU.subtract)
+
+        put(0)
+        put(1)
+        answer(0)
+        put(2)
+        answer(1)
+        put(3)
+        answer(2)
+        answer(3)
+        for t in range(PACK):
+            differ(t)
+
+        hid = keep.tile([P, O, PACK], BF16, name="hid", align_bytes=64)
+        by_place = diff[:].rearrange("p t o -> p o t")
+        lo, hi = slice(0, O // 2), slice(O // 2, O)
+        nc.vector.scalar_tensor_tensor(hid[:, lo, :], by_place[:, lo, :], -1.0, by_place[:, lo, :], ALU.mult, ALU.max)
+        nc.scalar.activation(hid[:, hi, :], by_place[:, hi, :], mybir.ActivationFunctionType.Abs)
+        hw = keep.tile([P, O], U32, name="hw", align_bytes=64)
+        hs = keep.tile([P, O], U8, name="hs", align_bytes=64)
+        nc.vector.quantize_mx(hw[:].bitcast(E4M3), hs[:], hid[:].rearrange("p o t -> p (o t)"))
+
+        for i in range(N // P):
+            cols = slice(P * i, P * (i + 1))
+            p_ps = psum.tile([P, O], F32, name="p_ps%d" % i)
+            nc.tensor.matmul_mx(
+                p_ps[:], lhsT=vgw[:, cols].bitcast(E5M2), lhsT_scale=vgs[:, cols],
+                rhs=hw[:].bitcast(E4M3), rhs_scale=hs[:], start=True, stop=True,
+            )
+            p_sb = keep.tile([P, O], F32, name="p_sb%d" % i)
+            if i == 0:
+                nc.vector.tensor_copy(p_sb[:], p_ps[:])
+                nc.vector.tensor_copy(pages[i][:].indirect(l7[:]), p_sb[:])
+                nc.sync.dma_start(out[cols, :], pages[i][:])
+            else:
+                nc.scalar.copy(p_sb[:], p_ps[:])
+                nc.scalar.activation(pages[i][:].indirect(l7[:]), p_sb[:], COPY)
+                nc.scalar.dma_start(out[cols, :], pages[i][:])

@@ -30,9 +30,15 @@ def load_list(nc, pool, src, name):
 
 
 def load_scale_rows(nc, pool, scales, name):
-    rows = pool.tile([PACK, QUADS, scales.shape[2] // 4], I32, name=name)
+    rows = pool.tile([PACK, QUADS, scales.shape[2] // 4], I32, name=name, tag=name)
     nc.sync.dma_start(rows[:], scales[0].bitcast(I32).rearrange("(q r) n -> r q n", r=PACK))
     return rows
+
+
+def load_scale_plane(nc, plane, scales):
+    rows = scales[0].bitcast(I32).rearrange("(q r) n -> r q n", r=PACK)
+    for r in range(PACK):
+        nc.sync.dma_start(plane[r:P:QUAD, :].bitcast(I32), rows[r])
 
 
 def spread_scale_rows(nc, plane, rows):
@@ -49,53 +55,57 @@ def tile_list_ownanswer_twow_store_scattered_kernel(
         keep = ctx.enter_context(tc.tile_pool(name="keep", bufs=1))
         psum = ctx.enter_context(tc.psum_pool(name="psum", bufs=1))
 
-        xs = keep.tile([P, T], U8, name="xs", align_bytes=64)
+        xs = keep.tile([P, T], U8, name="xs", tag="xs", align_bytes=64)
         ws = keep.tile([P, R], U8, name="ws", align_bytes=64)
-        boards = [keep.tile([P, C], F32, name="board%d" % t) for t in range(PACK)]
+        w2s = keep.tile([P, R], U8, name="w2s", tag="chain_v0", align_bytes=64)
+        vss = keep.tile([P, S], U8, name="vss", tag="vss", align_bytes=64)
+        boards = [keep.tile([P, C], F32, name="board%d" % u, tag="board%d" % u) for u in range(2)]
         nc.vector.memset(xs[:].bitcast(I32), 0)
         nc.vector.memset(ws[:].bitcast(I32), 0)
+        nc.vector.memset(w2s[:].bitcast(I32), 0)
+        nc.vector.memset(vss[:].bitcast(I32), 0)
         nc.vector.memset(boards[0][:], 0.0)
-        for t in range(1, PACK):
-            nc.vector.memset(boards[t][:], 0.0)
+        nc.vector.memset(boards[1][:], 0.0)
 
-        xw = keep.tile([P, T], U32, name="xw", align_bytes=64)
-        nc.scalar.dma_start(xw[:].bitcast(I32), xt_words[0].rearrange("p n t -> p (n t)").bitcast(I32))
-        xs_rows = load_scale_rows(nc, keep, xt_scales, "xs_rows")
         ws_rows = load_scale_rows(nc, keep, w_scales, "ws_rows")
         l1 = load_list(nc, keep, offs, "l1")
-        ww = keep.tile([P, R], U16, name="ww", align_bytes=64)
+        ww = keep.tile([P, R], U16, name="ww", tag="chain_v1", align_bytes=64)
         nc.sync.dma_start(ww[:].bitcast(I32), w_words[0].bitcast(I32))
         l2 = load_list(nc, keep, offs2, "l2")
         l3 = load_list(nc, keep, offs3, "l3")
-        sa_t = keep.tile([P, PACK], F32, name="sa_t")
-        nc.sync.dma_start(sa_t[:], sa.rearrange("(p t) o -> p (t o)", t=PACK))
-        w2s_rows = load_scale_rows(nc, keep, w2_scales, "w2s_rows")
-        w2w = keep.tile([P, R], U32, name="w2w", tag="wide1", align_bytes=64)
-        nc.sync.dma_start(w2w[:].bitcast(I32), w2_words[0].rearrange("p n t -> p (n t)").bitcast(I32))
-        vss_rows = load_scale_rows(nc, keep, vs_scales, "vss_rows")
-        l6 = load_list(nc, keep, offs6, "l6")
-        vw = keep.tile([P, S], U32, name="vw", tag="wide2", align_bytes=64)
-        nc.sync.dma_start(vw[:].bitcast(I32), vs_words[0].rearrange("p n t -> p (n t)").bitcast(I32))
         l4 = load_list(nc, keep, offs4, "l4")
+        xw = keep.tile([P, T], U32, name="xw", tag="wide2", align_bytes=64)
+        nc.sync.dma_start(xw[:].bitcast(I32), xt_words[0].rearrange("p n t -> p (n t)").bitcast(I32))
         l5 = load_list(nc, keep, offs5, "l5")
-        sb_t = keep.tile([P, PACK], F32, name="sb_t")
-        nc.sync.dma_start(sb_t[:], sb.rearrange("(p t) o -> p (t o)", t=PACK))
+        load_scale_plane(nc, xs, xt_scales)
+        l6 = load_list(nc, keep, offs6, "l6")
         l7 = load_list(nc, keep, offs7, "l7")
 
-        spread_scale_rows(nc, xs, xs_rows)
         spread_scale_rows(nc, ws, ws_rows)
         wsd = keep.tile([P, PACK, P], U8, name="wsd", tag="chain_s", align_bytes=64)
         nc.vector.tensor_copy(wsd[:], ws[:].rearrange("p (m t) -> p t m", t=PACK))
         wwd = keep.tile([P, PACK, P], U16, name="wwd", tag="chain_w", align_bytes=64)
         nc.scalar.copy(wwd[:], ww[:].rearrange("p (m t) -> p t m", t=PACK))
 
+        w2w = keep.tile([P, R], U32, name="w2w", tag="chain_v1", align_bytes=64)
+        nc.sync.dma_start(w2w[:].bitcast(I32), w2_words[0].rearrange("p n t -> p (n t)").bitcast(I32))
+        sa_t = keep.tile([P, PACK], F32, name="sa_t", tag="ws_rows")
+        nc.sync.dma_start(sa_t[:], sa.rearrange("(p t) o -> p (t o)", t=PACK))
+        load_scale_plane(nc, w2s, w2_scales)
+        load_scale_plane(nc, vss, vs_scales)
+
         xgs = keep.tile([P, J], U8, name="xgs", align_bytes=64)
         xgw = keep.tile([P, J], U32, name="xgw", align_bytes=64)
         half = J // 2
         halves = [(slice(0, half), slice(0, half // 16)), (slice(half, J), slice(half // 16, J // 16))]
         for cols, entries in halves:
-            nc.vector.tensor_copy(xgs[:, cols], xs[:].indirect(l1[:, entries]))
             nc.vector.tensor_copy(xgw[:, cols], xw[:].indirect(l1[:, entries]))
+            nc.vector.tensor_copy(xgs[:, cols], xs[:].indirect(l1[:, entries]))
+
+        vw = keep.tile([P, S], U32, name="vw", tag="wide2", align_bytes=64)
+        nc.sync.dma_start(vw[:].bitcast(I32), vs_words[0].rearrange("p n t -> p (n t)").bitcast(I32))
+        sb_t = keep.tile([P, PACK], F32, name="sb_t", tag="xs", align_bytes=64)
+        nc.sync.dma_start(sb_t[:], sb.rearrange("(p t) o -> p (t o)", t=PACK))
 
         a_sb = keep.tile([P, PACK, J], F32, name="a_sb")
 
@@ -117,10 +127,7 @@ def tile_list_ownanswer_twow_store_scattered_kernel(
             first_product(bank[:, t - 2, :], t, slice(0, J))
         nc.vector.tensor_copy(a_sb[:, 2:4, :], bank[:])
 
-        w2s = keep.tile([P, R], U8, name="w2s", tag="chain_s", align_bytes=64)
-        nc.vector.memset(w2s[:].bitcast(I32), 0)
-        spread_scale_rows(nc, w2s, w2s_rows)
-        w2sd = keep.tile([P, PACK, P], U8, name="w2sd", align_bytes=64)
+        w2sd = keep.tile([P, PACK, P], U8, name="w2sd", tag="chain_s", align_bytes=64)
         nc.vector.tensor_copy(w2sd[:], w2s[:].rearrange("p (m t) -> p t m", t=PACK))
         w2wd = keep.tile([P, PACK, P], U32, name="w2wd", tag="chain_w", align_bytes=64)
         nc.vector.tensor_copy(w2wd[:], w2w[:].rearrange("p (m t) -> p t m", t=PACK))
@@ -135,52 +142,52 @@ def tile_list_ownanswer_twow_store_scattered_kernel(
             b_ps.append(bank)
 
         pages = []
-        page0 = keep.tile([P, E], F32, name="page0", tag="chain_w", align_bytes=64)
-        nc.vector.memset(page0[:], 0.0)
-        pages.append(page0)
-        vgs = keep.tile([P, N], U8, name="vgs", align_bytes=64)
-        vgw = keep.tile([P, N], U32, name="vgw", tag="chain_s", align_bytes=64)
+        vgs = keep.tile([P, N], U8, name="vgs", tag="chain_v0", align_bytes=64)
+        vgw = keep.tile([P, N], U32, name="vgw", tag="chain_v1", align_bytes=64)
 
-        vss = keep.tile([P, S], U8, name="vss", tag="wide1", align_bytes=64)
-        nc.vector.memset(vss[:].bitcast(I32), 0)
-        spread_scale_rows(nc, vss, vss_rows)
         nc.vector.tensor_copy(vgs[:], vss[:].indirect(l6[:]))
         nc.vector.tensor_copy(vgw[:], vw[:].indirect(l6[:]))
 
-        page1 = keep.tile([P, E], F32, name="page1", tag="wide1", align_bytes=64)
-        nc.vector.memset(page1[:], 0.0)
-        pages.append(page1)
         first = keep.tile([P, PACK, O], F32, name="first")
-        second = keep.tile([P, PACK, O], F32, name="second")
         diff = keep.tile([P, PACK, O], F32, name="diff")
-        rb = [keep.tile([P, J], F32, name="rb0", tag="wide2", align_bytes=64)]
-        rb.extend(keep.tile([P, J], F32, name="rb%d" % t) for t in range(1, PACK))
+        rb = [
+            keep.tile([P, J], F32, name="rb%d" % t, tag=tag, align_bytes=64)
+            for t, tag in enumerate(("rb0", "rb1", "wide2", "vss"))
+        ]
 
         def put(t):
             if t == 0:
                 for cols, entries in halves:
-                    nc.scalar.activation(boards[t][:].indirect(l2[:, entries]), a_sb[:, t, cols], COPY)
+                    nc.scalar.activation(boards[t % 2][:].indirect(l2[:, entries]), a_sb[:, t, cols], COPY)
             else:
-                nc.scalar.activation(boards[t][:].indirect(l2[:]), a_sb[:, t, :], COPY)
+                nc.scalar.activation(boards[t % 2][:].indirect(l2[:]), a_sb[:, t, :], COPY)
 
         def answer(t):
-            looked = keep.tile([P, J], F32, name="looked%d" % t)
-            nc.scalar.activation(looked[:], boards[t][:].indirect(l3[:]), COPY, scale=sa_t[:, t : t + 1])
+            looked = keep.tile([P, J], F32, name="looked%d" % t, tag="looked%d" % t)
+            nc.scalar.activation(looked[:], boards[t % 2][:].indirect(l3[:]), COPY, scale=sa_t[:, t : t + 1])
             nc.vector.tensor_tensor(rb[t][:], b_ps[t], looked[:], ALU.max)
             nc.vector.tensor_copy(first[:, t, :], rb[t][:].indirect(l4[:]))
+            if t < N // P:
+                page = keep.tile([P, E], F32, name="page%d" % t, tag="looked%d" % t)
+                nc.vector.memset(page[:], 0.0)
+                pages.append(page)
 
         def differ(t):
             nc.scalar.activation(second[:, t, :], rb[t][:].indirect(l5[:]), COPY, scale=sb_t[:, t : t + 1])
-            nc.vector.tensor_tensor(diff[:, t, :], first[:, t, :], second[:, t, :], ALU.subtract)
+            if t == PACK - 2:
+                nc.vector.tensor_tensor(diff[:, : t + 1, :], first[:, : t + 1, :], second[:, : t + 1, :], ALU.subtract)
+            elif t == PACK - 1:
+                nc.vector.tensor_tensor(diff[:, t, :], first[:, t, :], second[:, t, :], ALU.subtract)
 
         put(0)
         put(1)
         answer(0)
-        put(2)
         answer(1)
+        put(2)
         put(3)
         answer(2)
         answer(3)
+        second = keep.tile([P, PACK, O], F32, name="second", tag="board1")
         for t in range(PACK):
             differ(t)
 

@@ -42,8 +42,10 @@ def load_scale_plane(nc, plane, scales):
 
 
 def spread_scale_rows(nc, plane, rows):
-    for q in range(QUADS):
-        nc.vector.tensor_copy(plane[QUAD * q : QUAD * q + PACK, :].bitcast(I32), rows[:, q, :])
+    words = plane[:].bitcast(I32).rearrange("p (h n) -> p h n", h=2)
+    for q in range(2):
+        nc.vector.tensor_copy(words[QUAD * q : QUAD * q + PACK], rows[:, q:QUADS:2, :])
+    nc.vector.tensor_copy(words[P // 2 :, 0, :], words[: P // 2, 1, :])
 
 
 def tile_list_ownanswer_twow_store_scattered_kernel(
@@ -56,11 +58,12 @@ def tile_list_ownanswer_twow_store_scattered_kernel(
         psum = ctx.enter_context(tc.psum_pool(name="psum", bufs=1))
 
         xs = keep.tile([P, T], U8, name="xs", tag="xs", align_bytes=64)
-        ws = keep.tile([P, R], U8, name="ws", align_bytes=64)
+        ws = keep.tile([P, 2 * R], U8, name="ws", align_bytes=64)
         w2s = keep.tile([P, R], U8, name="w2s", tag="chain_v0", align_bytes=64)
         vss = keep.tile([P, S], U8, name="vss", tag="vss", align_bytes=64)
         boards = [keep.tile([P, C], F32, name="board%d" % u, tag="board%d" % u) for u in range(2)]
-        nc.vector.memset(xs[:].bitcast(I32), 0)
+        nc.vector.memset(xs[:, : T // 2].bitcast(I32), 0)
+        nc.gpsimd.memset(xs[:, T // 2 :].bitcast(I32), 0)
         nc.vector.memset(ws[:].bitcast(I32), 0)
         nc.vector.memset(w2s[:].bitcast(I32), 0)
         nc.vector.memset(vss[:].bitcast(I32), 0)
@@ -71,19 +74,20 @@ def tile_list_ownanswer_twow_store_scattered_kernel(
         l1 = load_list(nc, keep, offs, "l1")
         ww = keep.tile([P, R], U16, name="ww", tag="chain_v1", align_bytes=64)
         nc.sync.dma_start(ww[:].bitcast(I32), w_words[0].bitcast(I32))
+        load_scale_plane(nc, xs, xt_scales)
+        xw = keep.tile([P, T], U32, name="xw", tag="wide2", align_bytes=64)
+        nc.sync.dma_start(xw[:].bitcast(I32), xt_words[0].rearrange("p n t -> p (n t)").bitcast(I32))
         l2 = load_list(nc, keep, offs2, "l2")
         l3 = load_list(nc, keep, offs3, "l3")
         l4 = load_list(nc, keep, offs4, "l4")
-        xw = keep.tile([P, T], U32, name="xw", tag="wide2", align_bytes=64)
-        nc.sync.dma_start(xw[:].bitcast(I32), xt_words[0].rearrange("p n t -> p (n t)").bitcast(I32))
         l5 = load_list(nc, keep, offs5, "l5")
-        load_scale_plane(nc, xs, xt_scales)
         l6 = load_list(nc, keep, offs6, "l6")
         l7 = load_list(nc, keep, offs7, "l7")
 
         spread_scale_rows(nc, ws, ws_rows)
-        wsd = keep.tile([P, PACK, P], U8, name="wsd", tag="chain_s", align_bytes=64)
-        nc.vector.tensor_copy(wsd[:], ws[:].rearrange("p (m t) -> p t m", t=PACK))
+        ws_by_tile = ws[:, :R].rearrange("p (m t) -> p t m", t=PACK)
+        wsd0 = keep.tile([P, P], U8, name="wsd0", tag="chain_s", align_bytes=64)
+        nc.vector.tensor_copy(wsd0[:], ws_by_tile[:, 0, :])
         wwd = keep.tile([P, PACK, P], U16, name="wwd", tag="chain_w", align_bytes=64)
         nc.scalar.copy(wwd[:], ww[:].rearrange("p (m t) -> p t m", t=PACK))
 
@@ -99,8 +103,8 @@ def tile_list_ownanswer_twow_store_scattered_kernel(
         half = J // 2
         halves = [(slice(0, half), slice(0, half // 16)), (slice(half, J), slice(half // 16, J // 16))]
         for cols, entries in halves:
-            nc.vector.tensor_copy(xgw[:, cols], xw[:].indirect(l1[:, entries]))
             nc.vector.tensor_copy(xgs[:, cols], xs[:].indirect(l1[:, entries]))
+            nc.vector.tensor_copy(xgw[:, cols], xw[:].indirect(l1[:, entries]))
 
         vw = keep.tile([P, S], U32, name="vw", tag="wide2", align_bytes=64)
         nc.sync.dma_start(vw[:].bitcast(I32), vs_words[0].rearrange("p n t -> p (n t)").bitcast(I32))
@@ -109,22 +113,24 @@ def tile_list_ownanswer_twow_store_scattered_kernel(
 
         a_sb = keep.tile([P, PACK, J], F32, name="a_sb")
 
-        def first_product(bank, t, cols):
+        def first_product(bank, t, cols, scale):
             nc.tensor.matmul_mx(
-                bank, lhsT=wwd[:, t, :].bitcast(E2M1), lhsT_scale=wsd[:, t, :],
+                bank, lhsT=wwd[:, t, :].bitcast(E2M1), lhsT_scale=scale,
                 rhs=xgw[:, cols].bitcast(E4M3), rhs_scale=xgs[:, cols], start=True, stop=True,
             )
 
         for u, (cols, entries) in enumerate(halves):
             bank = psum.tile([P, half], F32, name="a_ps0%d" % u)
-            first_product(bank[:], 0, cols)
+            first_product(bank[:], 0, cols, wsd0[:])
             nc.vector.tensor_copy(a_sb[:, 0, cols], bank[:])
+        wsd = keep.tile([P, PACK - 1, P], U8, name="wsd", tag="chain_s", align_bytes=64)
+        nc.vector.tensor_copy(wsd[:], ws_by_tile[:, 1:PACK, :])
         bank = psum.tile([P, J], F32, name="a_ps1")
-        first_product(bank[:], 1, slice(0, J))
+        first_product(bank[:], 1, slice(0, J), wsd[:, 0, :])
         nc.vector.tensor_copy(a_sb[:, 1, :], bank[:])
         bank = psum.tile([P, 2, J], F32, name="a_ps23")
         for t in (2, 3):
-            first_product(bank[:, t - 2, :], t, slice(0, J))
+            first_product(bank[:, t - 2, :], t, slice(0, J), wsd[:, t - 1, :])
         nc.vector.tensor_copy(a_sb[:, 2:4, :], bank[:])
 
         w2sd = keep.tile([P, PACK, P], U8, name="w2sd", tag="chain_s", align_bytes=64)
@@ -187,7 +193,7 @@ def tile_list_ownanswer_twow_store_scattered_kernel(
         put(3)
         answer(2)
         answer(3)
-        second = keep.tile([P, PACK, O], F32, name="second", tag="board1")
+        second = keep.tile([P, PACK, O], F32, name="second", tag="board0")
         for t in range(PACK):
             differ(t)
 

@@ -71,12 +71,12 @@ def tile_list_ownanswer_twow_store_scattered_kernel(
         nc.vector.memset(boards[1][:], 0.0)
 
         ws_rows = load_scale_rows(nc, keep, w_scales, "ws_rows")
+        xw = keep.tile([P, T], U32, name="xw", tag="wide2", align_bytes=64)
+        nc.scalar.dma_start(xw[:].bitcast(I32), xt_words[0].rearrange("p n t -> p (n t)").bitcast(I32))
         l1 = load_list(nc, keep, offs, "l1")
         ww = keep.tile([P, R], U16, name="ww", tag="chain_v1", align_bytes=64)
         nc.sync.dma_start(ww[:].bitcast(I32), w_words[0].bitcast(I32))
         load_scale_plane(nc, xs, xt_scales)
-        xw = keep.tile([P, T], U32, name="xw", tag="wide2", align_bytes=64)
-        nc.sync.dma_start(xw[:].bitcast(I32), xt_words[0].rearrange("p n t -> p (n t)").bitcast(I32))
         l2 = load_list(nc, keep, offs2, "l2")
         l3 = load_list(nc, keep, offs3, "l3")
         l4 = load_list(nc, keep, offs4, "l4")

from contextlib import ExitStack

import concourse.mybir as mybir

K, T, J, R, C, O, N, S, E = 512, 1024, 256, 512, 512, 128, 256, 1024, 1024
FLOPS = 2 * (2 * K * R * J + R * N * O)

F32 = mybir.dt.float32
BF16 = mybir.dt.bfloat16
I32 = mybir.dt.int32
U32 = mybir.dt.uint32
U16 = mybir.dt.uint16
U8 = mybir.dt.uint8
E4M3 = mybir.dt.float8_e4m3fn_x4
E5M2 = mybir.dt.float8_e5m2_x4
E2M1 = mybir.dt.float4_e2m1fn_x4
COPY = mybir.ActivationFunctionType.Copy
ALU = mybir.AluOpType

P = 128
PACK = 4
QUADS = 4
QUAD = 32


def load_list(nc, pool, src, name):
    t = pool.tile(list(src.shape), U16, name=name)
    nc.sync.dma_start(t[:], src)
    return t


def load_scale_rows(nc, pool, scales, name):
    rows = pool.tile([PACK, QUADS, scales.shape[2] // 4], I32, name=name, tag=name)
    nc.sync.dma_start(rows[:], scales[0].bitcast(I32).rearrange("(q r) n -> r q n", r=PACK))
    return rows


def load_scale_plane(nc, plane, scales):
    rows = scales[0].bitcast(I32).rearrange("(q r) n -> r q n", r=PACK)
    for r in range(PACK):
        nc.sync.dma_start(plane[r:P:QUAD, :].bitcast(I32), rows[r])


def spread_scale_rows(nc, plane, rows):
    words = plane[:].bitcast(I32).rearrange("p (h n) -> p h n", h=2)
    for q in range(2):
        nc.vector.tensor_copy(words[QUAD * q : QUAD * q + PACK], rows[:, q:QUADS:2, :])
    nc.vector.tensor_copy(words[P // 2 :, 0, :], words[: P // 2, 1, :])


def tile_list_ownanswer_twow_store_scattered_kernel(
    tc, xt_words, xt_scales, w_words, w_scales, w2_words, w2_scales, sa, sb, vs_words, vs_scales,
    offs, offs2, offs3, offs4, offs5, offs6, offs7, out,
):
    nc = tc.nc
    with ExitStack() as ctx:
        keep = ctx.enter_context(tc.tile_pool(name="keep", bufs=1))
        psum = ctx.enter_context(tc.psum_pool(name="psum", bufs=1))

        xs = keep.tile([P, T], U8, name="xs", tag="xs", align_bytes=64)
        ws = keep.tile([P, 2 * R], U8, name="ws", align_bytes=64)
        w2s = keep.tile([P, R], U8, name="w2s", tag="chain_v0", align_bytes=64)
        vss = keep.tile([P, S], U8, name="vss", tag="vss", align_bytes=64)
        boards = [keep.tile([P, C], F32, name="board%d" % u, tag="board%d" % u) for u in range(2)]
        nc.vector.memset(xs[:, : T // 2].bitcast(I32), 0)
        nc.gpsimd.memset(xs[:, T // 2 :].bitcast(I32), 0)
        nc.vector.memset(ws[:].bitcast(I32), 0)
        nc.vector.memset(w2s[:].bitcast(I32), 0)
        nc.vector.memset(vss[:].bitcast(I32), 0)
        nc.vector.memset(boards[0][:], 0.0)
        nc.vector.memset(boards[1][:], 0.0)

        ws_rows = load_scale_rows(nc, keep, w_scales, "ws_rows")
        xw = keep.tile([P, T], U32, name="xw", tag="wide2", align_bytes=64)
        nc.scalar.dma_start(xw[:].bitcast(I32), xt_words[0].rearrange("p n t -> p (n t)").bitcast(I32))
        l1 = load_list(nc, keep, offs, "l1")
        ww = keep.tile([P, R], U16, name="ww", tag="chain_v1", align_bytes=64)
        nc.sync.dma_start(ww[:].bitcast(I32), w_words[0].bitcast(I32))
        load_scale_plane(nc, xs, xt_scales)
        l2 = load_list(nc, keep, offs2, "l2")
        l3 = load_list(nc, keep, offs3, "l3")
        l4 = load_list(nc, keep, offs4, "l4")
        l5 = load_list(nc, keep, offs5, "l5")
        l6 = load_list(nc, keep, offs6, "l6")
        l7 = load_list(nc, keep, offs7, "l7")

        spread_scale_rows(nc, ws, ws_rows)
        ws_by_tile = ws[:, :R].rearrange("p (m t) -> p t m", t=PACK)
        wsd0 = keep.tile([P, P], U8, name="wsd0", tag="chain_s", align_bytes=64)
        nc.vector.tensor_copy(wsd0[:], ws_by_tile[:, 0, :])
        wwd = keep.tile([P, PACK, P], U16, name="wwd", tag="chain_w", align_bytes=64)
        nc.scalar.copy(wwd[:], ww[:].rearrange("p (m t) -> p t m", t=PACK))

        w2w = keep.tile([P, R], U32, name="w2w", tag="chain_v1", align_bytes=64)
        nc.sync.dma_start(w2w[:].bitcast(I32), w2_words[0].rearrange("p n t -> p (n t)").bitcast(I32))
        sa_t = keep.tile([P, PACK], F32, name="sa_t", tag="ws_rows")
        nc.sync.dma_start(sa_t[:], sa.rearrange("(p t) o -> p (t o)", t=PACK))
        load_scale_plane(nc, w2s, w2_scales)
        load_scale_plane(nc, vss, vs_scales)

        xgs = keep.tile([P, J], U8, name="xgs", align_bytes=64)
        xgw = keep.tile([P, J], U32, name="xgw", align_bytes=64)
        half = J // 2
        halves = [(slice(0, half), slice(0, half // 16)), (slice(half, J), slice(half // 16, J // 16))]
        for cols, entries in halves:
            nc.vector.tensor_copy(xgs[:, cols], xs[:].indirect(l1[:, entries]))
            nc.vector.tensor_copy(xgw[:, cols], xw[:].indirect(l1[:, entries]))

        vw = keep.tile([P, S], U32, name="vw", tag="wide2", align_bytes=64)
        nc.sync.dma_start(vw[:].bitcast(I32), vs_words[0].rearrange("p n t -> p (n t)").bitcast(I32))
        sb_t = keep.tile([P, PACK], F32, name="sb_t", tag="xs", align_bytes=64)
        nc.sync.dma_start(sb_t[:], sb.rearrange("(p t) o -> p (t o)", t=PACK))

        a_sb = keep.tile([P, PACK, J], F32, name="a_sb")

        def first_product(bank, t, cols, scale):
            nc.tensor.matmul_mx(
                bank, lhsT=wwd[:, t, :].bitcast(E2M1), lhsT_scale=scale,
                rhs=xgw[:, cols].bitcast(E4M3), rhs_scale=xgs[:, cols], start=True, stop=True,
            )

        for u, (cols, entries) in enumerate(halves):
            bank = psum.tile([P, half], F32, name="a_ps0%d" % u)
            first_product(bank[:], 0, cols, wsd0[:])
            nc.vector.tensor_copy(a_sb[:, 0, cols], bank[:])
        wsd = keep.tile([P, PACK - 1, P], U8, name="wsd", tag="chain_s", align_bytes=64)
        nc.vector.tensor_copy(wsd[:], ws_by_tile[:, 1:PACK, :])
        bank = psum.tile([P, J], F32, name="a_ps1")
        first_product(bank[:], 1, slice(0, J), wsd[:, 0, :])
        nc.vector.tensor_copy(a_sb[:, 1, :], bank[:])
        bank = psum.tile([P, 2, J], F32, name="a_ps23")
        for t in (2, 3):
            first_product(bank[:, t - 2, :], t, slice(0, J), wsd[:, t - 1, :])
        nc.vector.tensor_copy(a_sb[:, 2:4, :], bank[:])

        w2sd = keep.tile([P, PACK, P], U8, name="w2sd", tag="chain_s", align_bytes=64)
        nc.vector.tensor_copy(w2sd[:], w2s[:].rearrange("p (m t) -> p t m", t=PACK))
        w2wd = keep.tile([P, PACK, P], U32, name="w2wd", tag="chain_w", align_bytes=64)
        nc.vector.tensor_copy(w2wd[:], w2w[:].rearrange("p (m t) -> p t m", t=PACK))
        b_ps = []
        b_banks = [psum.tile([P, 2, J], F32, name="b_ps%d" % u) for u in range(2)]
        for t in range(PACK):
            bank = b_banks[t // 2][:, t % 2, :]
            nc.tensor.matmul_mx(
                bank, lhsT=w2wd[:, t, :].bitcast(E5M2), lhsT_scale=w2sd[:, t, :],
                rhs=xgw[:].bitcast(E4M3), rhs_scale=xgs[:], start=True, stop=True,
            )
            b_ps.append(bank)

        pages = []
        vgs = keep.tile([P, N], U8, name="vgs", tag="chain_v0", align_bytes=64)
        vgw = keep.tile([P, N], U32, name="vgw", tag="chain_v1", align_bytes=64)

        nc.vector.tensor_copy(vgs[:], vss[:].indirect(l6[:]))
        nc.vector.tensor_copy(vgw[:], vw[:].indirect(l6[:]))

        first = keep.tile([P, PACK, O], F32, name="first")
        diff = keep.tile([P, PACK, O], F32, name="diff")
        rb = [
            keep.tile([P, J], F32, name="rb%d" % t, tag=tag, align_bytes=64)
            for t, tag in enumerate(("rb0", "rb1", "wide2", "vss"))
        ]

        def put(t):
            if t == 0:
                for cols, entries in halves:
                    nc.scalar.activation(boards[t % 2][:].indirect(l2[:, entries]), a_sb[:, t, cols], COPY)
            else:
                nc.scalar.activation(boards[t % 2][:].indirect(l2[:]), a_sb[:, t, :], COPY)

        def answer(t):
            looked = keep.tile([P, J], F32, name="looked%d" % t, tag="looked%d" % t)
            nc.scalar.activation(looked[:], boards[t % 2][:].indirect(l3[:]), COPY, scale=sa_t[:, t : t + 1])
            nc.vector.tensor_tensor(rb[t][:], b_ps[t], looked[:], ALU.max)
            nc.vector.tensor_copy(first[:, t, :], rb[t][:].indirect(l4[:]))
            if t < N // P:
                page = keep.tile([P, E], F32, name="page%d" % t, tag="looked%d" % t)
                nc.vector.memset(page[:], 0.0)
                pages.append(page)

        def differ(t):
            nc.scalar.activation(second[:, t, :], rb[t][:].indirect(l5[:]), COPY, scale=sb_t[:, t : t + 1])
            if t == PACK - 2:
                nc.vector.tensor_tensor(diff[:, : t + 1, :], first[:, : t + 1, :], second[:, : t + 1, :], ALU.subtract)
            elif t == PACK - 1:
                nc.vector.tensor_tensor(diff[:, t, :], first[:, t, :], second[:, t, :], ALU.subtract)

        put(0)
        put(1)
        answer(0)
        answer(1)
        put(2)
        put(3)
        answer(2)
        answer(3)
        second = keep.tile([P, PACK, O], F32, name="second", tag="board0")
        for t in range(PACK):
            differ(t)

        hid = keep.tile([P, O, PACK], BF16, name="hid", align_bytes=64)
        by_place = diff[:].rearrange("p t o -> p o t")
        lo, hi = slice(0, O // 2), slice(O // 2, O)
        nc.vector.scalar_tensor_tensor(hid[:, lo, :], by_place[:, lo, :], -1.0, by_place[:, lo, :], ALU.mult, ALU.max)
        nc.scalar.activation(hid[:, hi, :], by_place[:, hi, :], mybir.ActivationFunctionType.Abs)
        hw = keep.tile([P, O], U32, name="hw", align_bytes=64)
        hs = keep.tile([P, O], U8, name="hs", align_bytes=64)
        nc.vector.quantize_mx(hw[:].bitcast(E4M3), hs[:], hid[:].rearrange("p o t -> p (o t)"))

        for i in range(N // P):
            cols = slice(P * i, P * (i + 1))
            p_ps = psum.tile([P, O], F32, name="p_ps%d" % i)
            nc.tensor.matmul_mx(
                p_ps[:], lhsT=vgw[:, cols].bitcast(E5M2), lhsT_scale=vgs[:, cols],
                rhs=hw[:].bitcast(E4M3), rhs_scale=hs[:], start=True, stop=True,
            )
            p_sb = keep.tile([P, O], F32, name="p_sb%d" % i)
            if i == 0:
                nc.vector.tensor_copy(p_sb[:], p_ps[:])
                nc.vector.tensor_copy(pages[i][:].indirect(l7[:]), p_sb[:])
                nc.sync.dma_start(out[cols, :], pages[i][:])
            else:
                nc.scalar.copy(p_sb[:], p_ps[:])
                nc.scalar.activation(pages[i][:].indirect(l7[:]), p_sb[:], COPY)
                nc.scalar.dma_start(out[cols, :], pages[i][:])
